import numpy as np
import ml_dtypes


def mxq(x, axis, fmt="e4m3"):
    dtype, down = {"e4m3": (ml_dtypes.float8_e4m3fn, 7), "e5m2": (ml_dtypes.float8_e5m2, 14)}[fmt]
    v = np.moveaxis(np.asarray(x, np.float32).astype(ml_dtypes.bfloat16).astype(np.float64), axis, -1)
    blocks = v.reshape(v.shape[:-1] + (-1, 32))
    amax = np.abs(blocks).max(-1, keepdims=True)
    byte = np.maximum(np.where(amax > 0, np.frexp(amax)[1] - 1 + 127, 0) - down, 1)
    scale = np.exp2(byte - 127.0)
    codes = (blocks / scale).astype(np.float32).astype(dtype).astype(np.float64)
    return np.moveaxis((codes * scale).reshape(v.shape), -1, axis)


WIDE = False


def mx_kscale(k):
    if not WIDE:
        return np.ones(k)
    levels = np.array([10, -10, 5, -5, 0])
    if k % 512:
        return np.exp2(np.random.permutation(np.resize(levels, k // 32))).repeat(32)
    a = np.empty((k // 512, 16))
    for p in range(k // 512):
        a[p, :8] = np.random.permutation(np.resize(levels, 8))
        for g in range(8):
            far = levels[np.abs(levels - a[p, g]) >= 10]
            a[p, g + 8] = far[np.random.randint(len(far))]
    return np.exp2(a.ravel()).repeat(32)


def f64(x):
    return np.asarray(x).astype(np.float64)


def striped(idx):
    return np.tile(idx.reshape(-1, 16).T, (8, 1)).astype(np.uint16)


def unstriped(offs):
    return offs[:16].T.reshape(-1).astype(np.int64)


def pack_weight(w):
    k, n = w.shape
    w = f64(np.asarray(w, np.float32).astype(ml_dtypes.bfloat16)).reshape(k // 32, 32, n)
    amax = np.abs(w).max(1)
    byte = np.clip(np.where(amax > 0, np.frexp(amax)[1] - 1 + 127 - 7, 1), 1, 254)
    scaled = (w * np.exp2(127.0 - byte)[:, None, :]).reshape(k, n).astype(np.float32)
    words = np.ascontiguousarray(scaled.reshape(k // 512, 128, 4, n).transpose(0, 1, 3, 2)).astype(ml_dtypes.float8_e4m3fn).view(np.uint8)
    return words, np.ascontiguousarray(byte.astype(np.uint8).reshape(k // 512, 16, n))


def unpack_weight(words, scales):
    g, p, n, _ = words.shape
    vals = np.ascontiguousarray(words).view(ml_dtypes.float8_e4m3fn).astype(np.float64) * np.repeat(np.exp2(scales.astype(np.float64) - 127.0), 8, axis=1)[..., None]
    return vals.transpose(0, 1, 3, 2).reshape(g * 512, n)


K, T, S, V = 512, 2048, 512, 512
P = 2 ** 7


def setup_inputs():
    n = np.random.standard_normal
    s = mx_kscale(K)[:, None]
    packed_xT = pack_weight(n((K, T)) * s)
    return {
        "x_words": packed_xT[0],
        "x_scales": packed_xT[1],
        "hT": (n((K, V)) / np.sqrt(K) / s).astype(np.float32),
        "nn": (np.tile(np.random.uniform(0.5, 2.0, T), (P, 1))).astype(np.float32),
        "own": (np.random.uniform(0.5, 1.5, (V, 1))).astype(np.float32),
        "isc": (np.tile(np.random.uniform(0.3, 0.9, T), (P, 1))).astype(np.float32),
        "shp": (np.tile(np.random.uniform(0.8, 2.5, T), (P, 1))).astype(np.float32),
        "offs": striped(np.random.permutation(T)[:S]),
    }


def reference(x_words, x_scales, hT, nn, own, isc, shp, offs):
    hTq = mxq(f64(hT), 0, "e4m3")
    xq = unpack_weight(x_words, x_scales)[:, unstriped(offs)]
    y = hTq.T @ xq
    dis = np.log(np.exp(f64(nn)[:1][:, unstriped(offs)] - y + f64(own)) + 1.0) + 0.1
    keep = np.exp(-1.0 * (np.exp((f64(shp)[:1][:, unstriped(offs)]) * (np.log(dis * (f64(isc)[:1][:, unstriped(offs)]))))))
    yr = y * keep
    er = np.exp(yr)
    tr = er.sum(axis=1, keepdims=True)
    yu = np.abs(y) * (-1.0 * keep + 1.0)
    unk = yu.mean(axis=1, keepdims=True)
    return 100.0 * (np.exp(yr) / ((tr + 1.0) * (0.2 * unk + 1.0)))

@@ -1,0 +1,232 @@
+import math
+from contextlib import ExitStack
+
+import concourse.mybir as mybir
+from concourse.masks import make_identity
+
+K, T, S, V = 512, 2048, 512, 512
+P = 128
+PACK = 4
+NB = V // P
+NJ = S // P
+
+FLOPS = 2 * K * V * S
+BYTES = K * T + (K // 32) * T + 4 * K * V + 3 * 4 * T + 4 * V + 2 * P * (S // 16) + 4 * V * S
+
+F32 = mybir.dt.float32
+BF16 = mybir.dt.bfloat16
+I32 = mybir.dt.int32
+U32 = mybir.dt.uint32
+U16 = mybir.dt.uint16
+U8 = mybir.dt.uint8
+FP8X4 = mybir.dt.float8_e4m3fn_x4
+ALU = mybir.AluOpType
+ACT = mybir.ActivationFunctionType
+AX = mybir.AxisListType
+
+SHIFT = 0.1
+LN_CAP = 2.0 ** 60
+UNK = 0.2 / S
+ROW = P - 3
+GROUPS = ((0,), (1,), (2, 3))
+
+
+def tile_picked_yopenm_prob_p_kernel(
+    tc, x_words, x_scales, hT, nn, own, isc, shp, offs, out
+):
+    nc = tc.nc
+    with ExitStack() as ctx:
+        sb = ctx.enter_context(tc.tile_pool(name="sb", bufs=1))
+        ps = ctx.enter_context(tc.psum_pool(name="ps", bufs=1))
+
+        def tiles(name, n, shape, dtype):
+            return [sb.tile(shape, dtype, name="%s%d" % (name, i), align_bytes=64) for i in range(n)]
+
+        offsets = sb.tile([P, S // 16], U16, name="offsets")
+        words_all = sb.tile([P, T], U32, name="words_all", align_bytes=64)
+        bytes_all = sb.tile([P, T], U8, name="bytes_all", align_bytes=64)
+        tables = sb.tile([P, T], F32, name="tables", align_bytes=64)
+        own_rows = sb.tile([P, P], F32, name="own_rows", align_bytes=64)
+        ident = sb.tile([P, P], F32, name="ident", align_bytes=64)
+        h_raw = tiles("h_raw", 2, [P, PACK, V // 2], F32)
+        y_ps = [ps.tile([P, S], F32, name="y_ps%d" % b) for b in range(NB)]
+        w_ps = [ps.tile([P, S], F32, name="w_ps%d" % b) for b in range(NB)]
+
+        nc.sync.dma_start(offsets[:], offs)
+        for r, table in enumerate((nn, isc, shp)):
+            nc.sync.dma_start(tables[ROW + r:ROW + r + 1, :], table[0:1, :])
+        nc.sync.dma_start(words_all[:].bitcast(I32), x_words[0].rearrange("p n t -> p (n t)").bitcast(I32))
+        nc.sync.dma_start(own_rows[P - NB:P, :], own.rearrange("(b p) o -> b (p o)", p=P))
+        h_view = hT.rearrange("(p j) w -> p j w", j=PACK)
+        for h in range(2):
+            nc.sync.dma_start(h_raw[h][:], h_view[:, :, h * (V // 2):(h + 1) * (V // 2)])
+        nc.vector.memset(tables[0:ROW, :], 0.0)
+        nc.gpsimd.memset(bytes_all[:].bitcast(I32), 0)
+        nc.gpsimd.memset(own_rows[0:P - NB, :], 0.0)
+        for q in range(4):
+            nc.scalar.dma_start(bytes_all[32 * q:32 * q + 4, :].bitcast(I32), x_scales[0, 4 * q:4 * q + 4, :].bitcast(I32))
+        make_identity(nc, ident[:])
+
+        picked = sb.tile([P, S], F32, name="picked", align_bytes=64)
+        x_codes = sb.tile([P, S], U32, name="x_codes", align_bytes=64)
+        x_bytes = sb.tile([P, S], U8, name="x_bytes", align_bytes=64)
+        nc.vector.tensor_copy(picked[:], tables[:].indirect(offsets[:]))
+        nc.vector.tensor_copy(x_bytes[:], bytes_all[:].indirect(offsets[:]))
+        nc.vector.tensor_copy(x_codes[:], words_all[:].indirect(offsets[:]))
+
+        cols = sb.tile([P, 3, NJ], F32, name="cols", align_bytes=64)
+        own_col = sb.tile([P, NB], F32, name="own_col", align_bytes=64)
+        nn_row = sb.tile([P, S], F32, name="nn_row", align_bytes=64)
+        for c in range(NJ):
+            nc.tensor.transpose(w_ps[0][:, c * P:(c + 1) * P], picked[:, c * P:(c + 1) * P], ident[:])
+        nc.scalar.copy(cols[:], w_ps[0][:].rearrange("p (c r) -> p r c", c=NJ)[:, ROW:P, :])
+        for c in range(NJ):
+            nc.tensor.transpose(w_ps[2][:, c * P:(c + 1) * P], cols[:, 0, c:c + 1].to_broadcast([P, P]), ident[:])
+        nc.scalar.copy(nn_row[:], w_ps[2][:])
+        nc.tensor.transpose(w_ps[1][:, 0:P], own_rows[:], ident[:])
+        nc.scalar.activation(own_col[:], w_ps[1][:, P - NB:P], ACT.Identity, bias=SHIFT)
+
+        h_bf = tiles("h_bf", NB, [P, P, PACK], BF16)
+        h_codes = tiles("h_codes", NB, [P, P], U32)
+        h_bytes = tiles("h_bytes", NB, [P, P], U8)
+        neg_a = sb.tile([P, NB, S], F32, name="neg_a", align_bytes=64)
+        exp_a = sb.tile([P, NB, S], F32, name="exp_a", align_bytes=64)
+        for b in range(NB):
+            src = h_raw[b // 2][:, :, (b % 2) * P:(b % 2 + 1) * P].rearrange("p j w -> p w j")
+            if b != 1:
+                nc.scalar.copy(h_bf[b][:], src)
+            else:
+                nc.vector.tensor_copy(h_bf[b][:], src)
+            nc.vector.quantize_mx(
+                out=h_codes[b][:].bitcast(FP8X4), scales=h_bytes[b][:], in_=h_bf[b][:].rearrange("p w j -> p (w j)")
+            )
+            nc.tensor.matmul_mx(
+                out=y_ps[b][:],
+                lhsT=h_codes[b][:].bitcast(FP8X4),
+                lhsT_scale=h_bytes[b][:],
+                rhs=x_codes[:].bitcast(FP8X4),
+                rhs_scale=x_bytes[:],
+                start=True,
+                stop=True,
+            )
+            nc.vector.scalar_tensor_tensor(
+                neg_a[:, b, :], y_ps[b][:], own_col[:, b:b + 1], nn_row[:], ALU.subtract, ALU.subtract
+            )
+            nc.scalar.activation(exp_a[:, b, :], neg_a[:, b, :], ACT.Exp, scale=-1.0)
+
+        capped = tiles("capped", NJ, [P, NB, P], F32)
+        soft = tiles("soft", NJ, [P, NB, P], F32)
+        dis = tiles("dis", NJ, [P, S + NJ], F32)
+        log_dis = tiles("log_dis", NJ, [P, S + NJ], F32)
+        nc.vector.tensor_copy(dis[0][:, S:S + NJ], cols[:, 1, :])
+        for c in range(NJ):
+            nc.vector.tensor_scalar(capped[c][:], exp_a[:, :, c * P:(c + 1) * P], LN_CAP, None, ALU.min)
+        for c in range(NJ):
+            nc.scalar.activation(soft[c][:], capped[c][:], ACT.Ln, bias=math.exp(SHIFT))
+            nc.vector.scalar_tensor_tensor(
+                dis[c][:, 0:S].rearrange("p (b j) -> p b j", b=NB),
+                neg_a[:, :, c * P:(c + 1) * P], -1.0, soft[c][:], ALU.mult, ALU.max,
+            )
+
+        def turned(b, c):
+            group = [g for g in GROUPS if b in g][0]
+            per_bank = NJ // len(group)
+            bank = group[c // per_bank]
+            start = (c % per_bank) * len(group) * P + group.index(b) * P
+            return bank, start
+
+        for c in range(NJ):
+            width = S + NJ if c == 0 else S
+            nc.scalar.activation(log_dis[c][:, 0:width], dis[c][:, 0:width], ACT.Ln)
+            for b in range(NB):
+                bank, start = turned(b, c)
+                nc.tensor.transpose(w_ps[bank][:, start:start + P], log_dis[c][:, b * P:(b + 1) * P], ident[:])
+        law_bias = sb.tile([P, NJ], F32, name="law_bias", align_bytes=64)
+        nc.vector.tensor_tensor(law_bias[:], log_dis[0][:, S:S + NJ], cols[:, 2, :], ALU.mult)
+
+        pos = sb.tile([P, NB], F32, name="pos", align_bytes=64)
+        neg = sb.tile([P, NB], F32, name="neg", align_bytes=64)
+        base = sb.tile([P, NB], F32, name="base", align_bytes=64)
+        for b in range(NB):
+            nc.vector.tensor_scalar(exp_a[:, b, :], y_ps[b][:], 0.0, None, ALU.max, ALU.add, accum_out=pos[:, b:b + 1])
+            nc.vector.tensor_scalar(capped[b][:].rearrange("p b j -> p (b j)"), y_ps[b][:], 0.0, None, ALU.min, ALU.add, accum_out=neg[:, b:b + 1])
+        nc.vector.tensor_tensor(base[:], pos[:], neg[:], ALU.subtract)
+        nc.vector.tensor_scalar(base[:], base[:], 0.01 * UNK, 0.01, ALU.mult, ALU.add)
+
+        power = tiles("power", NJ, [P, V], F32)
+        keep = tiles("keep", NB, [P, S], F32)
+        yr = tiles("yr", NB, [P, S + 8], F32)
+        er = tiles("er", NB, [P, S + 8], F32)
+        res = tiles("res", NB, [P, S], F32)
+        neg_max = tiles("neg_max", NB, [P, 1], F32)
+        total = tiles("total", NB, [P, 1], F32)
+        abs_sum = tiles("abs_sum", NB, [P, 1], F32)
+        unknown = tiles("unknown", NB, [P, 1], F32)
+        inv_unknown = tiles("inv_unknown", NB, [P, 1], F32)
+        inv_total = tiles("inv_total", NB, [P, 1], F32)
+        for b in range(NB):
+            nc.gpsimd.memset(yr[b][:, S:S + 8], 0.0)
+
+        def law_power(group):
+            width = len(group) * P
+            for c in range(NJ):
+                bank, start = turned(group[0], c)
+                nc.scalar.activation(
+                    power[c][:, group[0] * P:group[0] * P + width], w_ps[bank][:, start:start + width], ACT.Exp,
+                    scale=cols[:, 2, c:c + 1], bias=law_bias[:, c:c + 1],
+                )
+            for b in group:
+                for c in range(NJ):
+                    nc.tensor.transpose(w_ps[b][:, c * P:(c + 1) * P], power[c][:, b * P:(b + 1) * P], ident[:])
+
+        def keep_share(b):
+            nc.scalar.activation(keep[b][:], w_ps[b][:], ACT.Exp, scale=-1.0)
+
+        def kept_scores(b):
+            nc.vector.tensor_tensor(yr[b][:, 0:S], y_ps[b][:], keep[b][:], ALU.mult)
+            nc.vector.tensor_scalar(
+                dis[b][:, 0:S], yr[b][:, 0:S], -1.0, 0.0, ALU.mult, ALU.min, accum_out=neg_max[b][:]
+            )
+
+        def unknown_share(b):
+            if b in (1, 2):
+                nc.scalar.activation(keep[b][:], yr[b][:, 0:S], ACT.Abs, accum_out=abs_sum[b][:])
+            else:
+                nc.vector.tensor_reduce(abs_sum[b][:], yr[b][:, 0:S], AX.X, ALU.add, apply_absolute_value=True)
+            nc.vector.tensor_scalar(unknown[b][:], abs_sum[b][:], -0.01 * UNK, base[:, b:b + 1], ALU.mult, ALU.add)
+
+        def exponentials(b):
+            nc.scalar.activation(
+                er[b][:, 0:S + 1], yr[b][:, 0:S + 1], ACT.Exp, bias=neg_max[b][:], accum_out=total[b][:]
+            )
+
+        def chances(b):
+            if b == NB - 1:
+                nc.vector.reciprocal(inv_unknown[b][:], unknown[b][:])
+                nc.vector.reciprocal(inv_total[b][:], total[b][:])
+                nc.vector.tensor_scalar(
+                    res[b][:], er[b][:, 0:S], inv_unknown[b][:], inv_total[b][:], ALU.mult, ALU.mult
+                )
+            else:
+                nc.vector.tensor_tensor(inv_unknown[b][:], unknown[b][:], total[b][:], ALU.mult)
+                nc.vector.reciprocal(inv_total[b][:], inv_unknown[b][:])
+                nc.gpsimd.tensor_scalar(res[b][:], er[b][:, 0:S], inv_total[b][:], 0.0, ALU.mult, ALU.add)
+            nc.sync.dma_start(out[b * P:(b + 1) * P, :], res[b][:])
+
+        law_power(GROUPS[0])
+        law_power(GROUPS[1])
+        keep_share(0)
+        kept_scores(0)
+        unknown_share(0)
+        law_power(GROUPS[2])
+        for b in range(1, NB):
+            keep_share(b)
+        for b in range(1, NB):
+            kept_scores(b)
+            exponentials(b - 1)
+            if b > 1:
+                unknown_share(b - 1)
+            chances(b - 1)
+        exponentials(NB - 1)
+        unknown_share(NB - 1)
+        chances(NB - 1)

@@ -27,7 +27,6 @@ AX = mybir.AxisListType
 SHIFT = 0.1
 LN_CAP = 2.0 ** 60
 UNK = 0.2 / S
-ROW = P - 3
 GROUPS = ((0,), (1,), (2, 3))
 
 
@@ -43,119 +42,114 @@ def tile_picked_yopenm_prob_p_kernel(
             return [sb.tile(shape, dtype, name="%s%d" % (name, i), align_bytes=64) for i in range(n)]
 
         offsets = sb.tile([P, S // 16], U16, name="offsets")
-        words_all = sb.tile([P, T], U32, name="words_all", align_bytes=64)
+        words_all = sb.tile([P, T], U32, name="words_all", tag="words", align_bytes=64)
         bytes_all = sb.tile([P, T], U8, name="bytes_all", align_bytes=64)
-        tables = sb.tile([P, T], F32, name="tables", align_bytes=64)
-        own_rows = sb.tile([P, P], F32, name="own_rows", align_bytes=64)
+        tables = sb.tile([P, T], F32, name="tables", tag="tables", align_bytes=64)
+        own_col = sb.tile([P, NB], F32, name="own_col", tag="own_col", align_bytes=64)
         ident = sb.tile([P, P], F32, name="ident", align_bytes=64)
-        h_raw = tiles("h_raw", 2, [P, PACK, V // 2], F32)
+        h_raw = [
+            sb.tile([P, PACK, V // 2], F32, name="h_raw%d" % h, tag="h_raw%d" % h, align_bytes=64) for h in range(2)
+        ]
         y_ps = [ps.tile([P, S], F32, name="y_ps%d" % b) for b in range(NB)]
         w_ps = [ps.tile([P, S], F32, name="w_ps%d" % b) for b in range(NB)]
 
-        nc.sync.dma_start(offsets[:], offs)
-        for r, table in enumerate((nn, isc, shp)):
-            nc.sync.dma_start(tables[ROW + r:ROW + r + 1, :], table[0:1, :])
-        nc.sync.dma_start(words_all[:].bitcast(I32), x_words[0].rearrange("p n t -> p (n t)").bitcast(I32))
-        nc.sync.dma_start(own_rows[P - NB:P, :], own.rearrange("(b p) o -> b (p o)", p=P))
-        h_view = hT.rearrange("(p j) w -> p j w", j=PACK)
-        for h in range(2):
-            nc.sync.dma_start(h_raw[h][:], h_view[:, :, h * (V // 2):(h + 1) * (V // 2)])
-        nc.vector.memset(tables[0:ROW, :], 0.0)
-        nc.gpsimd.memset(bytes_all[:].bitcast(I32), 0)
-        nc.gpsimd.memset(own_rows[0:P - NB, :], 0.0)
-        for q in range(4):
-            nc.scalar.dma_start(bytes_all[32 * q:32 * q + 4, :].bitcast(I32), x_scales[0, 4 * q:4 * q + 4, :].bitcast(I32))
+        warm = sb.tile([P, 2], F32, name="warm", align_bytes=64)
+        nc.vector.memset(bytes_all[:].bitcast(I32), 0)
+        nc.vector.memset(warm[:, 0:1], 0.0)
+        nc.scalar.activation(warm[:, 1:2], warm[:, 0:1], ACT.Exp)
+        nc.vector.memset(tables[:], 0.0)
         make_identity(nc, ident[:])
+        nc.sync.dma_start(offsets[:], offs)
+        nc.sync.dma_start(own_col[:], own.rearrange("(p b) o -> p (b o)", b=NB))
+        for q in range(4):
+            nc.sync.dma_start(bytes_all[32 * q:32 * q + 4, :].bitcast(I32), x_scales[0, 4 * q:4 * q + 4, :].bitcast(I32))
+        h_view = hT.rearrange("(p j) w -> p j w", j=PACK)
+        nc.sync.dma_start(h_raw[0][:], h_view[:, :, 0:V // 2])
+        nc.sync.dma_start(words_all[:].bitcast(I32), x_words[0].rearrange("p n t -> p (n t)").bitcast(I32))
+        nc.sync.dma_start(h_raw[1][:], h_view[:, :, V // 2:V])
+        for r, table in enumerate((nn, isc, shp)):
+            nc.scalar.dma_start(tables[8 + 4 * r:9 + 4 * r, :], table[0:1, :])
 
-        picked = sb.tile([P, S], F32, name="picked", align_bytes=64)
         x_codes = sb.tile([P, S], U32, name="x_codes", align_bytes=64)
         x_bytes = sb.tile([P, S], U8, name="x_bytes", align_bytes=64)
-        nc.vector.tensor_copy(picked[:], tables[:].indirect(offsets[:]))
         nc.vector.tensor_copy(x_bytes[:], bytes_all[:].indirect(offsets[:]))
         nc.vector.tensor_copy(x_codes[:], words_all[:].indirect(offsets[:]))
+        picked = sb.tile([P, S], F32, name="picked", tag="words", align_bytes=64)
+        nc.vector.tensor_copy(picked[:], tables[:].indirect(offsets[:]))
 
-        cols = sb.tile([P, 3, NJ], F32, name="cols", align_bytes=64)
-        own_col = sb.tile([P, NB], F32, name="own_col", align_bytes=64)
-        nn_row = sb.tile([P, S], F32, name="nn_row", align_bytes=64)
-        for c in range(NJ):
-            nc.tensor.transpose(w_ps[0][:, c * P:(c + 1) * P], picked[:, c * P:(c + 1) * P], ident[:])
-        nc.scalar.copy(cols[:], w_ps[0][:].rearrange("p (c r) -> p r c", c=NJ)[:, ROW:P, :])
-        for c in range(NJ):
-            nc.tensor.transpose(w_ps[2][:, c * P:(c + 1) * P], cols[:, 0, c:c + 1].to_broadcast([P, P]), ident[:])
-        nc.scalar.copy(nn_row[:], w_ps[2][:])
-        nc.tensor.transpose(w_ps[1][:, 0:P], own_rows[:], ident[:])
-        nc.scalar.activation(own_col[:], w_ps[1][:, P - NB:P], ACT.Identity, bias=SHIFT)
+        own_row = sb.tile([P, NB, P], F32, name="own_row", align_bytes=64)
+        for b in range(NB):
+            nc.tensor.transpose(y_ps[b][:, 0:P], own_col[:, b:b + 1].to_broadcast([P, P]), ident[:])
+            nc.scalar.activation(own_row[:, b, :], y_ps[b][:, 0:P], ACT.Identity, bias=SHIFT)
 
-        h_bf = tiles("h_bf", NB, [P, P, PACK], BF16)
+        h_early = tiles("h_early", 2, [P, P, PACK], BF16)
+        h_late = sb.tile([P, 2, P, PACK], BF16, name="h_late", tag="own_col", align_bytes=64)
+        h_bf = [h_early[0][:], h_early[1][:], h_late[:, 0, :, :], h_late[:, 1, :, :]]
         h_codes = tiles("h_codes", NB, [P, P], U32)
         h_bytes = tiles("h_bytes", NB, [P, P], U8)
-        neg_a = sb.tile([P, NB, S], F32, name="neg_a", align_bytes=64)
-        exp_a = sb.tile([P, NB, S], F32, name="exp_a", align_bytes=64)
+        gap = sb.tile([P, NJ, V], F32, name="gap", tag="tables", align_bytes=64)
+        exp_a = tiles("exp_a", NJ, [P, V], F32)
         for b in range(NB):
             src = h_raw[b // 2][:, :, (b % 2) * P:(b % 2 + 1) * P].rearrange("p j w -> p w j")
-            if b != 1:
-                nc.scalar.copy(h_bf[b][:], src)
-            else:
-                nc.vector.tensor_copy(h_bf[b][:], src)
+            nc.scalar.copy(h_bf[b], src)
             nc.vector.quantize_mx(
-                out=h_codes[b][:].bitcast(FP8X4), scales=h_bytes[b][:], in_=h_bf[b][:].rearrange("p w j -> p (w j)")
+                out=h_codes[b][:].bitcast(FP8X4), scales=h_bytes[b][:], in_=h_bf[b].rearrange("p w j -> p (w j)")
             )
-            nc.tensor.matmul_mx(
-                out=y_ps[b][:],
-                lhsT=h_codes[b][:].bitcast(FP8X4),
-                lhsT_scale=h_bytes[b][:],
-                rhs=x_codes[:].bitcast(FP8X4),
-                rhs_scale=x_bytes[:],
-                start=True,
-                stop=True,
+            for c in range(NJ):
+                nc.tensor.matmul_mx(
+                    out=y_ps[b][:, c * P:(c + 1) * P],
+                    lhsT=x_codes[:, c * P:(c + 1) * P].bitcast(FP8X4),
+                    lhsT_scale=x_bytes[:, c * P:(c + 1) * P],
+                    rhs=h_codes[b][:].bitcast(FP8X4),
+                    rhs_scale=h_bytes[b][:],
+                    start=True,
+                    stop=True,
+                )
+            nc.vector.tensor_tensor(
+                gap[:, :, b * P:(b + 1) * P].rearrange("p c (m e) -> p c m e", e=NB),
+                own_row[:, :, b * 32:(b + 1) * 32].rearrange("p e m -> p m e").unsqueeze(1).to_broadcast([P, NJ, 32, NB]),
+                y_ps[b][:].rearrange("p (c m e) -> p c m e", c=NJ, e=NB),
+                ALU.subtract,
             )
-            nc.vector.scalar_tensor_tensor(
-                neg_a[:, b, :], y_ps[b][:], own_col[:, b:b + 1], nn_row[:], ALU.subtract, ALU.subtract
-            )
-            nc.scalar.activation(exp_a[:, b, :], neg_a[:, b, :], ACT.Exp, scale=-1.0)
-
-        capped = tiles("capped", NJ, [P, NB, P], F32)
-        soft = tiles("soft", NJ, [P, NB, P], F32)
-        dis = tiles("dis", NJ, [P, S + NJ], F32)
-        log_dis = tiles("log_dis", NJ, [P, S + NJ], F32)
-        nc.vector.tensor_copy(dis[0][:, S:S + NJ], cols[:, 1, :])
+        cols = sb.tile([P, 3, NJ], F32, name="cols", tag="h_raw1", align_bytes=64)
         for c in range(NJ):
-            nc.vector.tensor_scalar(capped[c][:], exp_a[:, :, c * P:(c + 1) * P], LN_CAP, None, ALU.min)
+            nc.tensor.transpose(w_ps[1][:, c * P:(c + 1) * P], picked[:, c * P:(c + 1) * P], ident[:])
+        nc.scalar.copy(cols[:], w_ps[1][:].rearrange("p (c r) -> p r c", c=NJ)[:, 8:20:4, :])
+        for samples in (slice(0, 2 * P), slice(2 * P, 3 * P), slice(3 * P, 4 * P)):
+            for c in range(NJ):
+                nc.scalar.activation(exp_a[c][:, samples], gap[:, c, samples], ACT.Exp, bias=cols[:, 0, c:c + 1])
+
+        capped = tiles("capped", NJ, [P, V], F32)
+        soft = tiles("soft", NJ, [P, V], F32)
+        dis = [sb.tile([P, V], F32, name="dis%d" % c, tag="dis%d" % c, align_bytes=64) for c in range(NJ)]
+        log_dis = tiles("log_dis", NJ, [P, V], F32)
+        for c in range(NJ):
+            nc.vector.tensor_scalar(capped[c][:], exp_a[c][:], LN_CAP, None, ALU.min)
         for c in range(NJ):
             nc.scalar.activation(soft[c][:], capped[c][:], ACT.Ln, bias=math.exp(SHIFT))
-            nc.vector.scalar_tensor_tensor(
-                dis[c][:, 0:S].rearrange("p (b j) -> p b j", b=NB),
-                neg_a[:, :, c * P:(c + 1) * P], -1.0, soft[c][:], ALU.mult, ALU.max,
-            )
-
-        def turned(b, c):
-            group = [g for g in GROUPS if b in g][0]
-            per_bank = NJ // len(group)
-            bank = group[c // per_bank]
-            start = (c % per_bank) * len(group) * P + group.index(b) * P
-            return bank, start
-
+            nc.vector.scalar_tensor_tensor(dis[c][:], gap[:, c, :], cols[:, 0, c:c + 1], soft[c][:], ALU.add, ALU.max)
         for c in range(NJ):
-            width = S + NJ if c == 0 else S
-            nc.scalar.activation(log_dis[c][:, 0:width], dis[c][:, 0:width], ACT.Ln)
-            for b in range(NB):
-                bank, start = turned(b, c)
-                nc.tensor.transpose(w_ps[bank][:, start:start + P], log_dis[c][:, b * P:(b + 1) * P], ident[:])
-        law_bias = sb.tile([P, NJ], F32, name="law_bias", align_bytes=64)
-        nc.vector.tensor_tensor(law_bias[:], log_dis[0][:, S:S + NJ], cols[:, 2, :], ALU.mult)
+            nc.scalar.activation(log_dis[c][:], dis[c][:], ACT.Ln, scale=cols[:, 1, c:c + 1])
 
-        pos = sb.tile([P, NB], F32, name="pos", align_bytes=64)
-        neg = sb.tile([P, NB], F32, name="neg", align_bytes=64)
+        abs_y = sb.tile([P, NB], F32, name="abs_y", align_bytes=64)
         base = sb.tile([P, NB], F32, name="base", align_bytes=64)
         for b in range(NB):
-            nc.vector.tensor_scalar(exp_a[:, b, :], y_ps[b][:], 0.0, None, ALU.max, ALU.add, accum_out=pos[:, b:b + 1])
-            nc.vector.tensor_scalar(capped[b][:].rearrange("p b j -> p (b j)"), y_ps[b][:], 0.0, None, ALU.min, ALU.add, accum_out=neg[:, b:b + 1])
-        nc.vector.tensor_tensor(base[:], pos[:], neg[:], ALU.subtract)
-        nc.vector.tensor_scalar(base[:], base[:], 0.01 * UNK, 0.01, ALU.mult, ALU.add)
+            nc.vector.tensor_scalar(exp_a[b][:], y_ps[b][:], 0.0, 2.0, ALU.max, ALU.mult)
+            nc.vector.tensor_tensor(capped[b][:], exp_a[b][:], y_ps[b][:], ALU.subtract)
+            for c in range(NJ):
+                nc.tensor.matmul(
+                    w_ps[NB - 1][:, b * P:(b + 1) * P], capped[b][:, c * P:(c + 1) * P], ident[:],
+                    start=(c == 0), stop=(c == NJ - 1), is_transpose=True,
+                )
+        nc.vector.tensor_reduce(abs_y[:], w_ps[NB - 1][:].rearrange("p (b j) -> p b j", b=NB), AX.X, ALU.add)
+        nc.vector.tensor_scalar(base[:], abs_y[:], 0.01 * UNK, 0.01, ALU.mult, ALU.add)
 
-        power = tiles("power", NJ, [P, V], F32)
+        power = sb.tile([P, NJ, V], F32, name="power", tag="dis%d" % (NJ - 1), align_bytes=64)
+        minus_one = sb.tile([P, 1], F32, name="minus_one", align_bytes=64)
+        nc.gpsimd.memset(minus_one[:], -1.0)
         keep = tiles("keep", NB, [P, S], F32)
-        yr = tiles("yr", NB, [P, S + 8], F32)
+        kept = tiles("kept", NB, [P, S], F32)
+        neg_yr = tiles("neg_yr", NB, [P, S + 8], F32)
         er = tiles("er", NB, [P, S + 8], F32)
         res = tiles("res", NB, [P, S], F32)
         neg_max = tiles("neg_max", NB, [P, 1], F32)
@@ -165,68 +159,61 @@ def tile_picked_yopenm_prob_p_kernel(
         inv_unknown = tiles("inv_unknown", NB, [P, 1], F32)
         inv_total = tiles("inv_total", NB, [P, 1], F32)
         for b in range(NB):
-            nc.gpsimd.memset(yr[b][:, S:S + 8], 0.0)
+            nc.gpsimd.memset(neg_yr[b][:, S:S + 8], 0.0)
 
-        def law_power(group):
-            width = len(group) * P
+        def law(g):
+            group = GROUPS[g]
+            samples = slice(group[0] * P, (group[-1] + 1) * P)
             for c in range(NJ):
-                bank, start = turned(group[0], c)
-                nc.scalar.activation(
-                    power[c][:, group[0] * P:group[0] * P + width], w_ps[bank][:, start:start + width], ACT.Exp,
-                    scale=cols[:, 2, c:c + 1], bias=law_bias[:, c:c + 1],
-                )
+                nc.scalar.activation(power[:, c, samples], log_dis[c][:, samples], ACT.Exp, scale=cols[:, 2, c:c + 1])
             for b in group:
-                for c in range(NJ):
-                    nc.tensor.transpose(w_ps[b][:, c * P:(c + 1) * P], power[c][:, b * P:(b + 1) * P], ident[:])
-
-        def keep_share(b):
-            nc.scalar.activation(keep[b][:], w_ps[b][:], ACT.Exp, scale=-1.0)
+                nc.scalar.activation(
+                    keep[b][:].rearrange("p (c t) -> p c t", c=NJ), power[:, :, b * P:(b + 1) * P], ACT.Exp, scale=-1.0
+                )
 
         def kept_scores(b):
-            nc.vector.tensor_tensor(yr[b][:, 0:S], y_ps[b][:], keep[b][:], ALU.mult)
+            nc.vector.tensor_tensor(kept[b][:], y_ps[b][:], keep[b][:], ALU.mult)
+            for c in range(NJ):
+                nc.tensor.transpose(w_ps[b][:, c * P:(c + 1) * P], kept[b][:, c * P:(c + 1) * P], ident[:])
+
+        def row_max(b):
             nc.vector.tensor_scalar(
-                dis[b][:, 0:S], yr[b][:, 0:S], -1.0, 0.0, ALU.mult, ALU.min, accum_out=neg_max[b][:]
+                neg_yr[b][:, 0:S], w_ps[b][:], -1.0, 0.0, ALU.mult, ALU.min, accum_out=neg_max[b][:]
             )
 
         def unknown_share(b):
-            if b in (1, 2):
-                nc.scalar.activation(keep[b][:], yr[b][:, 0:S], ACT.Abs, accum_out=abs_sum[b][:])
+            if b < 2:
+                nc.scalar.activation(keep[b][:], neg_yr[b][:, 0:S], ACT.Abs, accum_out=abs_sum[b][:])
             else:
-                nc.vector.tensor_reduce(abs_sum[b][:], yr[b][:, 0:S], AX.X, ALU.add, apply_absolute_value=True)
-            nc.vector.tensor_scalar(unknown[b][:], abs_sum[b][:], -0.01 * UNK, base[:, b:b + 1], ALU.mult, ALU.add)
+                nc.vector.tensor_reduce(abs_sum[b][:], neg_yr[b][:, 0:S], AX.X, ALU.add, apply_absolute_value=True)
+            engine = nc.gpsimd if b < 2 else nc.vector
+            engine.tensor_scalar(unknown[b][:], abs_sum[b][:], -0.01 * UNK, base[:, b:b + 1], ALU.mult, ALU.add)
 
         def exponentials(b):
             nc.scalar.activation(
-                er[b][:, 0:S + 1], yr[b][:, 0:S + 1], ACT.Exp, bias=neg_max[b][:], accum_out=total[b][:]
+                er[b][:, 0:S + 1], neg_yr[b][:, 0:S + 1], ACT.Exp, scale=-1.0, bias=neg_max[b][:],
+                accum_out=total[b][:],
             )
 
         def chances(b):
-            if b == NB - 1:
+            if b >= 2:
                 nc.vector.reciprocal(inv_unknown[b][:], unknown[b][:])
                 nc.vector.reciprocal(inv_total[b][:], total[b][:])
                 nc.vector.tensor_scalar(
                     res[b][:], er[b][:, 0:S], inv_unknown[b][:], inv_total[b][:], ALU.mult, ALU.mult
                 )
             else:
-                nc.vector.tensor_tensor(inv_unknown[b][:], unknown[b][:], total[b][:], ALU.mult)
-                nc.vector.reciprocal(inv_total[b][:], inv_unknown[b][:])
+                nc.gpsimd.tensor_tensor(inv_unknown[b][:], unknown[b][:], total[b][:], ALU.mult)
+                nc.gpsimd.tensor_tensor(inv_total[b][:], inv_unknown[b][:], minus_one[:], ALU.pow)
                 nc.gpsimd.tensor_scalar(res[b][:], er[b][:, 0:S], inv_total[b][:], 0.0, ALU.mult, ALU.add)
             nc.sync.dma_start(out[b * P:(b + 1) * P, :], res[b][:])
 
-        law_power(GROUPS[0])
-        law_power(GROUPS[1])
-        keep_share(0)
-        kept_scores(0)
-        unknown_share(0)
-        law_power(GROUPS[2])
-        for b in range(1, NB):
-            keep_share(b)
-        for b in range(1, NB):
+        for g in range(len(GROUPS)):
+            law(g)
+        for b in range(NB):
             kept_scores(b)
-            exponentials(b - 1)
-            if b > 1:
-                unknown_share(b - 1)
-            chances(b - 1)
-        exponentials(NB - 1)
-        unknown_share(NB - 1)
-        chances(NB - 1)
+            row_max(b)
+        for b in range(NB):
+            exponentials(b)
+            unknown_share(b)
+            chances(b)

@@ -64,11 +64,11 @@ def tile_picked_yopenm_prob_p_kernel(
         for q in range(4):
             nc.sync.dma_start(bytes_all[32 * q:32 * q + 4, :].bitcast(I32), x_scales[0, 4 * q:4 * q + 4, :].bitcast(I32))
         h_view = hT.rearrange("(p j) w -> p j w", j=PACK)
-        nc.sync.dma_start(h_raw[0][:], h_view[:, :, 0:V // 2])
         nc.sync.dma_start(words_all[:].bitcast(I32), x_words[0].rearrange("p n t -> p (n t)").bitcast(I32))
-        nc.sync.dma_start(h_raw[1][:], h_view[:, :, V // 2:V])
         for r, table in enumerate((nn, isc, shp)):
-            nc.scalar.dma_start(tables[8 + 4 * r:9 + 4 * r, :], table[0:1, :])
+            nc.sync.dma_start(tables[8 + 4 * r:9 + 4 * r, :], table[0:1, :])
+        nc.sync.dma_start(h_raw[0][:], h_view[:, :, 0:V // 2])
+        nc.sync.dma_start(h_raw[1][:], h_view[:, :, V // 2:V])
 
         x_codes = sb.tile([P, S], U32, name="x_codes", align_bytes=64)
         x_bytes = sb.tile([P, S], U8, name="x_bytes", align_bytes=64)
@@ -77,38 +77,42 @@ def tile_picked_yopenm_prob_p_kernel(
         picked = sb.tile([P, S], F32, name="picked", tag="words", align_bytes=64)
         nc.vector.tensor_copy(picked[:], tables[:].indirect(offsets[:]))
 
-        own_row = sb.tile([P, NB, P], F32, name="own_row", align_bytes=64)
-        for b in range(NB):
-            nc.tensor.transpose(y_ps[b][:, 0:P], own_col[:, b:b + 1].to_broadcast([P, P]), ident[:])
-            nc.scalar.activation(own_row[:, b, :], y_ps[b][:, 0:P], ACT.Identity, bias=SHIFT)
+        own_row = sb.tile([P, V], F32, name="own_row", align_bytes=64)
+        for e in range(NB):
+            nc.tensor.transpose(y_ps[0][:, e * P:(e + 1) * P], own_col[:, e:e + 1].to_broadcast([P, P]), ident[:])
+        nc.scalar.activation(
+            own_row[:].rearrange("q (m e) -> q m e", e=NB), y_ps[0][:].rearrange("q (e m) -> q m e", e=NB),
+            ACT.Identity, bias=SHIFT,
+        )
 
-        h_early = tiles("h_early", 2, [P, P, PACK], BF16)
-        h_late = sb.tile([P, 2, P, PACK], BF16, name="h_late", tag="own_col", align_bytes=64)
-        h_bf = [h_early[0][:], h_early[1][:], h_late[:, 0, :, :], h_late[:, 1, :, :]]
-        h_codes = tiles("h_codes", NB, [P, P], U32)
+        h_first = sb.tile([P, P, PACK], BF16, name="h_first", align_bytes=64)
+        h_rest = sb.tile([P, NB - 1, P, PACK], BF16, name="h_rest", tag="own_col", align_bytes=64)
+        h_bf = [h_first[:]] + [h_rest[:, i, :, :] for i in range(NB - 1)]
+        h_codes = sb.tile([P, NB, P], U32, name="h_codes", tag="tables", align_bytes=64)
         h_bytes = tiles("h_bytes", NB, [P, P], U8)
-        gap = sb.tile([P, NJ, V], F32, name="gap", tag="tables", align_bytes=64)
+        gap = sb.tile([P, NJ, V], F32, name="gap", align_bytes=64)
         exp_a = tiles("exp_a", NJ, [P, V], F32)
         for b in range(NB):
             src = h_raw[b // 2][:, :, (b % 2) * P:(b % 2 + 1) * P].rearrange("p j w -> p w j")
             nc.scalar.copy(h_bf[b], src)
             nc.vector.quantize_mx(
-                out=h_codes[b][:].bitcast(FP8X4), scales=h_bytes[b][:], in_=h_bf[b].rearrange("p w j -> p (w j)")
+                out=h_codes[:, b, :].bitcast(FP8X4), scales=h_bytes[b][:], in_=h_bf[b].rearrange("p w j -> p (w j)")
             )
             for c in range(NJ):
                 nc.tensor.matmul_mx(
                     out=y_ps[b][:, c * P:(c + 1) * P],
                     lhsT=x_codes[:, c * P:(c + 1) * P].bitcast(FP8X4),
                     lhsT_scale=x_bytes[:, c * P:(c + 1) * P],
-                    rhs=h_codes[b][:].bitcast(FP8X4),
+                    rhs=h_codes[:, b, :].bitcast(FP8X4),
                     rhs_scale=h_bytes[b][:],
                     start=True,
                     stop=True,
                 )
+        for b in range(NB):
             nc.vector.tensor_tensor(
-                gap[:, :, b * P:(b + 1) * P].rearrange("p c (m e) -> p c m e", e=NB),
-                own_row[:, :, b * 32:(b + 1) * 32].rearrange("p e m -> p m e").unsqueeze(1).to_broadcast([P, NJ, 32, NB]),
-                y_ps[b][:].rearrange("p (c m e) -> p c m e", c=NJ, e=NB),
+                gap[:, :, b * P:(b + 1) * P],
+                own_row[:, b * P:(b + 1) * P].unsqueeze(1).to_broadcast([P, NJ, P]),
+                y_ps[b][:].rearrange("p (c t) -> p c t", c=NJ),
                 ALU.subtract,
             )
         cols = sb.tile([P, 3, NJ], F32, name="cols", tag="h_raw1", align_bytes=64)

@@ -7,8 +7,9 @@ from concourse.masks import make_identity
 K, T, S, V = 512, 2048, 512, 512
 P = 128
 PACK = 4
-NB = V // P
-NJ = S // P
+BLOCKS = V // P
+CHUNKS = S // P
+HALF = V // 2
 
 FLOPS = 2 * K * V * S
 BYTES = K * T + (K // 32) * T + 4 * K * V + 3 * 4 * T + 4 * V + 2 * P * (S // 16) + 4 * V * S
@@ -22,12 +23,16 @@ U8 = mybir.dt.uint8
 FP8X4 = mybir.dt.float8_e4m3fn_x4
 ALU = mybir.AluOpType
 ACT = mybir.ActivationFunctionType
-AX = mybir.AxisListType
+AXIS = mybir.AxisListType
 
 SHIFT = 0.1
 LN_CAP = 2.0 ** 60
 UNK = 0.2 / S
-GROUPS = ((0,), (1,), (2, 3))
+TABLE_ROWS = slice(8, 20, 4)
+VECTOR_ROUNDED_BLOCK = 1
+LAW_GROUPS = ((0,), (1,), (2, 3))
+EARLY_BLOCKS = 2
+PAD = 8
 
 
 def tile_picked_yopenm_prob_p_kernel(
@@ -38,186 +43,192 @@ def tile_picked_yopenm_prob_p_kernel(
         sb = ctx.enter_context(tc.tile_pool(name="sb", bufs=1))
         ps = ctx.enter_context(tc.psum_pool(name="ps", bufs=1))
 
-        def tiles(name, n, shape, dtype):
-            return [sb.tile(shape, dtype, name="%s%d" % (name, i), align_bytes=64) for i in range(n)]
+        def tile(name, shape, dtype, tag=None):
+            return sb.tile(shape, dtype, name=name, tag=tag or name, align_bytes=64)
+
+        def tiles(name, count, shape, dtype):
+            return [tile("%s%d" % (name, i), shape, dtype) for i in range(count)]
+
+        def span(i):
+            return slice(i * P, (i + 1) * P)
 
         offsets = sb.tile([P, S // 16], U16, name="offsets")
-        words_all = sb.tile([P, T], U32, name="words_all", tag="words", align_bytes=64)
-        bytes_all = sb.tile([P, T], U8, name="bytes_all", align_bytes=64)
-        tables = sb.tile([P, T], F32, name="tables", tag="tables", align_bytes=64)
-        own_col = sb.tile([P, NB], F32, name="own_col", tag="own_col", align_bytes=64)
-        ident = sb.tile([P, P], F32, name="ident", align_bytes=64)
-        h_raw = [
-            sb.tile([P, PACK, V // 2], F32, name="h_raw%d" % h, tag="h_raw%d" % h, align_bytes=64) for h in range(2)
-        ]
-        y_ps = [ps.tile([P, S], F32, name="y_ps%d" % b) for b in range(NB)]
-        w_ps = [ps.tile([P, S], F32, name="w_ps%d" % b) for b in range(NB)]
+        all_words = tile("all_words", [P, T], U32)
+        all_bytes = tile("all_bytes", [P, T], U8)
+        tables = tile("tables", [P, T], F32)
+        own_col = tile("own_col", [P, BLOCKS], F32)
+        ident = tile("ident", [P, P], F32)
+        h_raw = tiles("h_raw", 2, [P, PACK, HALF], F32)
+        y_ps = [ps.tile([P, S], F32, name="y_ps%d" % b) for b in range(BLOCKS)]
+        turn_ps = [ps.tile([P, S], F32, name="turn_ps%d" % b) for b in range(BLOCKS)]
 
-        warm = sb.tile([P, 2], F32, name="warm", align_bytes=64)
-        nc.vector.memset(bytes_all[:].bitcast(I32), 0)
-        nc.vector.memset(warm[:, 0:1], 0.0)
-        nc.scalar.activation(warm[:, 1:2], warm[:, 0:1], ACT.Exp)
+        nc.vector.memset(all_bytes[:].bitcast(I32), 0)
         nc.vector.memset(tables[:], 0.0)
         make_identity(nc, ident[:])
         nc.sync.dma_start(offsets[:], offs)
-        nc.sync.dma_start(own_col[:], own.rearrange("(p b) o -> p (b o)", b=NB))
+        nc.sync.dma_start(own_col[:], own.rearrange("(p e) o -> p (e o)", e=BLOCKS))
         for q in range(4):
-            nc.sync.dma_start(bytes_all[32 * q:32 * q + 4, :].bitcast(I32), x_scales[0, 4 * q:4 * q + 4, :].bitcast(I32))
+            nc.sync.dma_start(
+                all_bytes[32 * q:32 * q + 4, :].bitcast(I32), x_scales[0, 4 * q:4 * q + 4, :].bitcast(I32)
+            )
         h_view = hT.rearrange("(p j) w -> p j w", j=PACK)
-        nc.sync.dma_start(words_all[:].bitcast(I32), x_words[0].rearrange("p n t -> p (n t)").bitcast(I32))
-        for r, table in enumerate((nn, isc, shp)):
-            nc.sync.dma_start(tables[8 + 4 * r:9 + 4 * r, :], table[0:1, :])
-        nc.sync.dma_start(h_raw[0][:], h_view[:, :, 0:V // 2])
-        nc.sync.dma_start(h_raw[1][:], h_view[:, :, V // 2:V])
+        nc.sync.dma_start(all_words[:].bitcast(I32), x_words[0].rearrange("p n t -> p (n t)").bitcast(I32))
+        nc.sync.dma_start(h_raw[0][:], h_view[:, :, 0:HALF])
+        for row, table in zip(range(TABLE_ROWS.start, TABLE_ROWS.stop, TABLE_ROWS.step), (nn, isc, shp)):
+            nc.sync.dma_start(tables[row:row + 1, :], table[0:1, :])
+        nc.sync.dma_start(h_raw[1][:], h_view[:, :, HALF:V])
 
-        x_codes = sb.tile([P, S], U32, name="x_codes", align_bytes=64)
-        x_bytes = sb.tile([P, S], U8, name="x_bytes", align_bytes=64)
-        nc.vector.tensor_copy(x_bytes[:], bytes_all[:].indirect(offsets[:]))
-        nc.vector.tensor_copy(x_codes[:], words_all[:].indirect(offsets[:]))
-        picked = sb.tile([P, S], F32, name="picked", tag="words", align_bytes=64)
+        x_codes = tile("x_codes", [P, S], U32)
+        x_bytes = tile("x_bytes", [P, S], U8)
+        nc.vector.tensor_copy(x_bytes[:], all_bytes[:].indirect(offsets[:]))
+        nc.vector.tensor_copy(x_codes[:], all_words[:].indirect(offsets[:]))
+        picked = tile("picked", [P, S], F32, tag="all_words")
         nc.vector.tensor_copy(picked[:], tables[:].indirect(offsets[:]))
 
-        own_row = sb.tile([P, V], F32, name="own_row", align_bytes=64)
-        for e in range(NB):
-            nc.tensor.transpose(y_ps[0][:, e * P:(e + 1) * P], own_col[:, e:e + 1].to_broadcast([P, P]), ident[:])
+        own_row = tile("own_row", [P, V], F32)
+        for e in range(BLOCKS):
+            nc.tensor.transpose(y_ps[0][:, span(e)], own_col[:, e:e + 1].to_broadcast([P, P]), ident[:])
         nc.scalar.activation(
-            own_row[:].rearrange("q (m e) -> q m e", e=NB), y_ps[0][:].rearrange("q (e m) -> q m e", e=NB),
-            ACT.Identity, bias=SHIFT,
+            own_row[:].rearrange("q (m e) -> q m e", e=BLOCKS),
+            y_ps[0][:].rearrange("q (e m) -> q m e", e=BLOCKS),
+            ACT.Identity,
+            bias=SHIFT,
         )
 
-        h_first = sb.tile([P, P, PACK], BF16, name="h_first", align_bytes=64)
-        h_rest = sb.tile([P, NB - 1, P, PACK], BF16, name="h_rest", tag="own_col", align_bytes=64)
-        h_bf = [h_first[:]] + [h_rest[:, i, :, :] for i in range(NB - 1)]
-        h_codes = sb.tile([P, NB, P], U32, name="h_codes", tag="tables", align_bytes=64)
-        h_bytes = tiles("h_bytes", NB, [P, P], U8)
-        gap = sb.tile([P, NJ, V], F32, name="gap", align_bytes=64)
-        exp_a = tiles("exp_a", NJ, [P, V], F32)
-        for b in range(NB):
-            src = h_raw[b // 2][:, :, (b % 2) * P:(b % 2 + 1) * P].rearrange("p j w -> p w j")
-            nc.scalar.copy(h_bf[b], src)
+        h_bf = tiles("h_bf", BLOCKS, [P, P, PACK], BF16)
+        h_codes = tile("h_codes", [P, BLOCKS, P], U32)
+        h_bytes = tile("h_bytes", [P, BLOCKS, P], U8, tag="own_col")
+        for b in range(BLOCKS):
+            rows = h_raw[b // 2][:, :, span(b % 2)].rearrange("p j w -> p w j")
+            if b == VECTOR_ROUNDED_BLOCK:
+                nc.vector.tensor_copy(h_bf[b][:], rows)
+            else:
+                nc.scalar.copy(h_bf[b][:], rows)
             nc.vector.quantize_mx(
-                out=h_codes[:, b, :].bitcast(FP8X4), scales=h_bytes[b][:], in_=h_bf[b].rearrange("p w j -> p (w j)")
+                out=h_codes[:, b, :].bitcast(FP8X4),
+                scales=h_bytes[:, b, :],
+                in_=h_bf[b][:].rearrange("p w j -> p (w j)"),
             )
-            for c in range(NJ):
+            for c in range(CHUNKS):
                 nc.tensor.matmul_mx(
-                    out=y_ps[b][:, c * P:(c + 1) * P],
-                    lhsT=x_codes[:, c * P:(c + 1) * P].bitcast(FP8X4),
-                    lhsT_scale=x_bytes[:, c * P:(c + 1) * P],
+                    out=y_ps[b][:, span(c)],
+                    lhsT=x_codes[:, span(c)].bitcast(FP8X4),
+                    lhsT_scale=x_bytes[:, span(c)],
                     rhs=h_codes[:, b, :].bitcast(FP8X4),
-                    rhs_scale=h_bytes[b][:],
+                    rhs_scale=h_bytes[:, b, :],
                     start=True,
                     stop=True,
                 )
-        for b in range(NB):
+
+        gap = tile("gap", [P, CHUNKS, V], F32, tag="tables")
+        for b in range(BLOCKS):
             nc.vector.tensor_tensor(
-                gap[:, :, b * P:(b + 1) * P],
-                own_row[:, b * P:(b + 1) * P].unsqueeze(1).to_broadcast([P, NJ, P]),
-                y_ps[b][:].rearrange("p (c t) -> p c t", c=NJ),
+                gap[:, :, span(b)],
+                own_row[:, span(b)].unsqueeze(1).to_broadcast([P, CHUNKS, P]),
+                y_ps[b][:].rearrange("p (c t) -> p c t", c=CHUNKS),
                 ALU.subtract,
             )
-        cols = sb.tile([P, 3, NJ], F32, name="cols", tag="h_raw1", align_bytes=64)
-        for c in range(NJ):
-            nc.tensor.transpose(w_ps[1][:, c * P:(c + 1) * P], picked[:, c * P:(c + 1) * P], ident[:])
-        nc.scalar.copy(cols[:], w_ps[1][:].rearrange("p (c r) -> p r c", c=NJ)[:, 8:20:4, :])
-        for samples in (slice(0, 2 * P), slice(2 * P, 3 * P), slice(3 * P, 4 * P)):
-            for c in range(NJ):
-                nc.scalar.activation(exp_a[c][:, samples], gap[:, c, samples], ACT.Exp, bias=cols[:, 0, c:c + 1])
 
-        capped = tiles("capped", NJ, [P, V], F32)
-        soft = tiles("soft", NJ, [P, V], F32)
-        dis = [sb.tile([P, V], F32, name="dis%d" % c, tag="dis%d" % c, align_bytes=64) for c in range(NJ)]
-        log_dis = tiles("log_dis", NJ, [P, V], F32)
-        for c in range(NJ):
+        law = tile("law", [P, 3, CHUNKS], F32, tag="h_raw1")
+        for c in range(CHUNKS):
+            nc.tensor.transpose(turn_ps[1][:, span(c)], picked[:, span(c)], ident[:])
+        nc.scalar.copy(law[:], turn_ps[1][:].rearrange("p (c r) -> p r c", c=CHUNKS)[:, TABLE_ROWS, :])
+        nn_col = [law[:, 0, c:c + 1] for c in range(CHUNKS)]
+        isc_col = [law[:, 1, c:c + 1] for c in range(CHUNKS)]
+        shp_col = [law[:, 2, c:c + 1] for c in range(CHUNKS)]
+
+        exp_a = tiles("exp_a", CHUNKS, [P, V], F32)
+        for b in range(BLOCKS):
+            for c in range(CHUNKS):
+                nc.scalar.activation(exp_a[c][:, span(b)], gap[:, c, span(b)], ACT.Exp, bias=nn_col[c])
+
+        capped = tiles("capped", CHUNKS, [P, V], F32)
+        soft = tiles("soft", CHUNKS, [P, V], F32)
+        dis = tiles("dis", CHUNKS, [P, V], F32)
+        log_dis = tiles("log_dis", CHUNKS, [P, V], F32)
+        for c in range(CHUNKS):
             nc.vector.tensor_scalar(capped[c][:], exp_a[c][:], LN_CAP, None, ALU.min)
-        for c in range(NJ):
+        for c in range(CHUNKS):
             nc.scalar.activation(soft[c][:], capped[c][:], ACT.Ln, bias=math.exp(SHIFT))
-            nc.vector.scalar_tensor_tensor(dis[c][:], gap[:, c, :], cols[:, 0, c:c + 1], soft[c][:], ALU.add, ALU.max)
-        for c in range(NJ):
-            nc.scalar.activation(log_dis[c][:], dis[c][:], ACT.Ln, scale=cols[:, 1, c:c + 1])
+            nc.vector.scalar_tensor_tensor(dis[c][:], gap[:, c, :], nn_col[c], soft[c][:], ALU.add, ALU.max)
+        for c in range(CHUNKS):
+            nc.scalar.activation(log_dis[c][:], dis[c][:], ACT.Ln, scale=isc_col[c])
 
-        abs_y = sb.tile([P, NB], F32, name="abs_y", align_bytes=64)
-        base = sb.tile([P, NB], F32, name="base", align_bytes=64)
-        for b in range(NB):
-            nc.vector.tensor_scalar(exp_a[b][:], y_ps[b][:], 0.0, 2.0, ALU.max, ALU.mult)
-            nc.vector.tensor_tensor(capped[b][:], exp_a[b][:], y_ps[b][:], ALU.subtract)
-            for c in range(NJ):
+        twice_pos = tile("twice_pos", [P, BLOCKS, S], F32, tag="own_row")
+        abs_y_sum = tile("abs_y_sum", [P, BLOCKS], F32)
+        base = tile("base", [P, BLOCKS], F32)
+        sum_ps = turn_ps[BLOCKS - 1]
+        for b in range(BLOCKS):
+            abs_y = tile("abs_y%d" % b, [P, S], F32, tag="capped%d" % b)
+            nc.vector.tensor_scalar(twice_pos[:, b, :], y_ps[b][:], 0.0, 2.0, ALU.max, ALU.mult)
+            nc.vector.tensor_tensor(abs_y[:], twice_pos[:, b, :], y_ps[b][:], ALU.subtract)
+            for c in range(CHUNKS):
                 nc.tensor.matmul(
-                    w_ps[NB - 1][:, b * P:(b + 1) * P], capped[b][:, c * P:(c + 1) * P], ident[:],
-                    start=(c == 0), stop=(c == NJ - 1), is_transpose=True,
+                    sum_ps[:, span(b)], abs_y[:, span(c)], ident[:],
+                    start=(c == 0), stop=(c == CHUNKS - 1), is_transpose=True,
                 )
-        nc.vector.tensor_reduce(abs_y[:], w_ps[NB - 1][:].rearrange("p (b j) -> p b j", b=NB), AX.X, ALU.add)
-        nc.vector.tensor_scalar(base[:], abs_y[:], 0.01 * UNK, 0.01, ALU.mult, ALU.add)
+        nc.vector.tensor_reduce(
+            abs_y_sum[:], sum_ps[:].rearrange("p (b j) -> p b j", b=BLOCKS), AXIS.X, ALU.add
+        )
+        nc.vector.tensor_scalar(base[:], abs_y_sum[:], 1.0 / UNK, None, ALU.add)
 
-        power = sb.tile([P, NJ, V], F32, name="power", tag="dis%d" % (NJ - 1), align_bytes=64)
-        minus_one = sb.tile([P, 1], F32, name="minus_one", align_bytes=64)
-        nc.gpsimd.memset(minus_one[:], -1.0)
-        keep = tiles("keep", NB, [P, S], F32)
-        kept = tiles("kept", NB, [P, S], F32)
-        neg_yr = tiles("neg_yr", NB, [P, S + 8], F32)
-        er = tiles("er", NB, [P, S + 8], F32)
-        res = tiles("res", NB, [P, S], F32)
-        neg_max = tiles("neg_max", NB, [P, 1], F32)
-        total = tiles("total", NB, [P, 1], F32)
-        abs_sum = tiles("abs_sum", NB, [P, 1], F32)
-        unknown = tiles("unknown", NB, [P, 1], F32)
-        inv_unknown = tiles("inv_unknown", NB, [P, 1], F32)
-        inv_total = tiles("inv_total", NB, [P, 1], F32)
-        for b in range(NB):
-            nc.gpsimd.memset(neg_yr[b][:, S:S + 8], 0.0)
-
-        def law(g):
-            group = GROUPS[g]
+        power = tile("power", [P, CHUNKS, V], F32, tag="dis%d" % (CHUNKS - 1))
+        keep = tiles("keep", BLOCKS, [P, S], F32)
+        for group in LAW_GROUPS:
             samples = slice(group[0] * P, (group[-1] + 1) * P)
-            for c in range(NJ):
-                nc.scalar.activation(power[:, c, samples], log_dis[c][:, samples], ACT.Exp, scale=cols[:, 2, c:c + 1])
+            for c in range(CHUNKS):
+                nc.scalar.activation(power[:, c, samples], log_dis[c][:, samples], ACT.Exp, scale=shp_col[c])
             for b in group:
                 nc.scalar.activation(
-                    keep[b][:].rearrange("p (c t) -> p c t", c=NJ), power[:, :, b * P:(b + 1) * P], ACT.Exp, scale=-1.0
+                    keep[b][:].rearrange("p (c t) -> p c t", c=CHUNKS), power[:, :, span(b)], ACT.Exp, scale=-1.0
                 )
 
-        def kept_scores(b):
+        kept = tiles("kept", BLOCKS, [P, S], F32)
+        neg_yr = tiles("neg_yr", BLOCKS, [P, S + PAD], F32)
+        neg_max = tiles("neg_max", BLOCKS, [P, 1], F32)
+        minus_one = tile("minus_one", [P, 1], F32)
+        nc.gpsimd.memset(minus_one[:], -1.0)
+        for b in range(BLOCKS):
+            nc.gpsimd.memset(neg_yr[b][:, S:S + 1], 0.0)
+        for b in range(BLOCKS):
             nc.vector.tensor_tensor(kept[b][:], y_ps[b][:], keep[b][:], ALU.mult)
-            for c in range(NJ):
-                nc.tensor.transpose(w_ps[b][:, c * P:(c + 1) * P], kept[b][:, c * P:(c + 1) * P], ident[:])
-
-        def row_max(b):
+            for c in range(CHUNKS):
+                nc.tensor.transpose(turn_ps[b][:, span(c)], kept[b][:, span(c)], ident[:])
             nc.vector.tensor_scalar(
-                neg_yr[b][:, 0:S], w_ps[b][:], -1.0, 0.0, ALU.mult, ALU.min, accum_out=neg_max[b][:]
+                neg_yr[b][:, 0:S], turn_ps[b][:], -1.0, 0.0, ALU.mult, ALU.min, accum_out=neg_max[b][:]
             )
 
-        def unknown_share(b):
-            if b < 2:
-                nc.scalar.activation(keep[b][:], neg_yr[b][:, 0:S], ACT.Abs, accum_out=abs_sum[b][:])
-            else:
-                nc.vector.tensor_reduce(abs_sum[b][:], neg_yr[b][:, 0:S], AX.X, ALU.add, apply_absolute_value=True)
-            engine = nc.gpsimd if b < 2 else nc.vector
-            engine.tensor_scalar(unknown[b][:], abs_sum[b][:], -0.01 * UNK, base[:, b:b + 1], ALU.mult, ALU.add)
-
-        def exponentials(b):
+        er = tiles("er", BLOCKS, [P, S + PAD], F32)
+        res = tiles("res", BLOCKS, [P, S], F32)
+        total = tiles("total", BLOCKS, [P, 1], F32)
+        abs_yr_sum = tiles("abs_yr_sum", BLOCKS, [P, 1], F32)
+        denom = tiles("denom", BLOCKS, [P, 1], F32)
+        inv_denom = tiles("inv_denom", BLOCKS, [P, 1], F32)
+        for b in range(BLOCKS):
+            early = b < EARLY_BLOCKS
+            finisher = nc.gpsimd if early else nc.vector
             nc.scalar.activation(
-                er[b][:, 0:S + 1], neg_yr[b][:, 0:S + 1], ACT.Exp, scale=-1.0, bias=neg_max[b][:],
-                accum_out=total[b][:],
+                er[b][:, 0:S + 1], neg_yr[b][:, 0:S + 1], ACT.Exp,
+                scale=-1.0, bias=neg_max[b][:], accum_out=total[b][:],
             )
-
-        def chances(b):
-            if b >= 2:
-                nc.vector.reciprocal(inv_unknown[b][:], unknown[b][:])
-                nc.vector.reciprocal(inv_total[b][:], total[b][:])
-                nc.vector.tensor_scalar(
-                    res[b][:], er[b][:, 0:S], inv_unknown[b][:], inv_total[b][:], ALU.mult, ALU.mult
-                )
+            if early:
+                abs_yr = tile("abs_yr%d" % b, [P, S], F32, tag="keep%d" % b)
+                nc.scalar.activation(abs_yr[:], neg_yr[b][:, 0:S], ACT.Abs, accum_out=abs_yr_sum[b][:])
             else:
-                nc.gpsimd.tensor_tensor(inv_unknown[b][:], unknown[b][:], total[b][:], ALU.mult)
-                nc.gpsimd.tensor_tensor(inv_total[b][:], inv_unknown[b][:], minus_one[:], ALU.pow)
-                nc.gpsimd.tensor_scalar(res[b][:], er[b][:, 0:S], inv_total[b][:], 0.0, ALU.mult, ALU.add)
-            nc.sync.dma_start(out[b * P:(b + 1) * P, :], res[b][:])
-
-        for g in range(len(GROUPS)):
-            law(g)
-        for b in range(NB):
-            kept_scores(b)
-            row_max(b)
-        for b in range(NB):
-            exponentials(b)
-            unknown_share(b)
-            chances(b)
+                nc.vector.tensor_reduce(
+                    abs_yr_sum[b][:], neg_yr[b][:, 0:S], AXIS.X, ALU.add, apply_absolute_value=True
+                )
+            finisher.tensor_scalar(
+                denom[b][:], base[:, b:b + 1], abs_yr_sum[b][:], total[b][:], ALU.subtract, ALU.mult
+            )
+            if early:
+                nc.gpsimd.tensor_tensor(inv_denom[b][:], denom[b][:], minus_one[:], ALU.pow)
+            else:
+                nc.vector.reciprocal(inv_denom[b][:], denom[b][:])
+            queues = (nc.sync, nc.scalar) if b == BLOCKS - 1 else (nc.sync,)
+            for i, queue in enumerate(queues):
+                classes = slice(i * S // len(queues), (i + 1) * S // len(queues))
+                finisher.tensor_scalar(
+                    res[b][:, classes], er[b][:, classes], inv_denom[b][:], 100.0 / UNK, ALU.mult, ALU.mult
+                )
+                queue.dma_start(out[span(b), classes], res[b][:, classes])

import math
from contextlib import ExitStack

import concourse.mybir as mybir
from concourse.masks import make_identity

K, T, S, V = 512, 2048, 512, 512
P = 128
PACK = 4
BLOCKS = V // P
CHUNKS = S // P
HALF = V // 2

FLOPS = 2 * K * V * S
BYTES = K * T + (K // 32) * T + 4 * K * V + 3 * 4 * T + 4 * V + 2 * P * (S // 16) + 4 * V * S

F32 = mybir.dt.float32
BF16 = mybir.dt.bfloat16
I32 = mybir.dt.int32
U32 = mybir.dt.uint32
U16 = mybir.dt.uint16
U8 = mybir.dt.uint8
FP8X4 = mybir.dt.float8_e4m3fn_x4
ALU = mybir.AluOpType
ACT = mybir.ActivationFunctionType
AXIS = mybir.AxisListType

SHIFT = 0.1
LN_CAP = 2.0 ** 60
UNK = 0.2 / S
TABLE_ROWS = slice(8, 20, 4)
VECTOR_ROUNDED_BLOCK = 1
LAW_GROUPS = ((0,), (1,), (2, 3))
EARLY_BLOCKS = 2
PAD = 8


def tile_picked_yopenm_prob_p_kernel(
    tc, x_words, x_scales, hT, nn, own, isc, shp, offs, out
):
    nc = tc.nc
    with ExitStack() as ctx:
        sb = ctx.enter_context(tc.tile_pool(name="sb", bufs=1))
        ps = ctx.enter_context(tc.psum_pool(name="ps", bufs=1))

        def tile(name, shape, dtype, tag=None):
            return sb.tile(shape, dtype, name=name, tag=tag or name, align_bytes=64)

        def tiles(name, count, shape, dtype):
            return [tile("%s%d" % (name, i), shape, dtype) for i in range(count)]

        def span(i):
            return slice(i * P, (i + 1) * P)

        offsets = sb.tile([P, S // 16], U16, name="offsets")
        all_words = tile("all_words", [P, T], U32)
        all_bytes = tile("all_bytes", [P, T], U8)
        tables = tile("tables", [P, T], F32)
        own_col = tile("own_col", [P, BLOCKS], F32)
        ident = tile("ident", [P, P], F32)
        h_raw = tiles("h_raw", 2, [P, PACK, HALF], F32)
        y_ps = [ps.tile([P, S], F32, name="y_ps%d" % b) for b in range(BLOCKS)]
        turn_ps = [ps.tile([P, S], F32, name="turn_ps%d" % b) for b in range(BLOCKS)]

        nc.vector.memset(all_bytes[:].bitcast(I32), 0)
        nc.vector.memset(tables[:], 0.0)
        make_identity(nc, ident[:])
        nc.sync.dma_start(offsets[:], offs)
        nc.sync.dma_start(own_col[:], own.rearrange("(p e) o -> p (e o)", e=BLOCKS))
        for q in range(4):
            nc.sync.dma_start(
                all_bytes[32 * q:32 * q + 4, :].bitcast(I32), x_scales[0, 4 * q:4 * q + 4, :].bitcast(I32)
            )
        h_view = hT.rearrange("(p j) w -> p j w", j=PACK)
        nc.sync.dma_start(all_words[:].bitcast(I32), x_words[0].rearrange("p n t -> p (n t)").bitcast(I32))
        nc.sync.dma_start(h_raw[0][:], h_view[:, :, 0:HALF])
        for row, table in zip(range(TABLE_ROWS.start, TABLE_ROWS.stop, TABLE_ROWS.step), (nn, isc, shp)):
            nc.sync.dma_start(tables[row:row + 1, :], table[0:1, :])
        nc.sync.dma_start(h_raw[1][:], h_view[:, :, HALF:V])

        x_codes = tile("x_codes", [P, S], U32)
        x_bytes = tile("x_bytes", [P, S], U8)
        nc.vector.tensor_copy(x_bytes[:], all_bytes[:].indirect(offsets[:]))
        nc.vector.tensor_copy(x_codes[:], all_words[:].indirect(offsets[:]))
        picked = tile("picked", [P, S], F32, tag="all_words")
        nc.vector.tensor_copy(picked[:], tables[:].indirect(offsets[:]))

        own_row = tile("own_row", [P, V], F32)
        for e in range(BLOCKS):
            nc.tensor.transpose(y_ps[0][:, span(e)], own_col[:, e:e + 1].to_broadcast([P, P]), ident[:])
        nc.scalar.activation(
            own_row[:].rearrange("q (m e) -> q m e", e=BLOCKS),
            y_ps[0][:].rearrange("q (e m) -> q m e", e=BLOCKS),
            ACT.Identity,
            bias=SHIFT,
        )

        h_bf = tiles("h_bf", BLOCKS, [P, P, PACK], BF16)
        h_codes = tile("h_codes", [P, BLOCKS, P], U32)
        h_bytes = tile("h_bytes", [P, BLOCKS, P], U8, tag="own_col")
        for b in range(BLOCKS):
            rows = h_raw[b // 2][:, :, span(b % 2)].rearrange("p j w -> p w j")
            if b == VECTOR_ROUNDED_BLOCK:
                nc.vector.tensor_copy(h_bf[b][:], rows)
            else:
                nc.scalar.copy(h_bf[b][:], rows)
            nc.vector.quantize_mx(
                out=h_codes[:, b, :].bitcast(FP8X4),
                scales=h_bytes[:, b, :],
                in_=h_bf[b][:].rearrange("p w j -> p (w j)"),
            )
            for c in range(CHUNKS):
                nc.tensor.matmul_mx(
                    out=y_ps[b][:, span(c)],
                    lhsT=x_codes[:, span(c)].bitcast(FP8X4),
                    lhsT_scale=x_bytes[:, span(c)],
                    rhs=h_codes[:, b, :].bitcast(FP8X4),
                    rhs_scale=h_bytes[:, b, :],
                    start=True,
                    stop=True,
                )

        gap = tile("gap", [P, CHUNKS, V], F32, tag="tables")
        for b in range(BLOCKS):
            nc.vector.tensor_tensor(
                gap[:, :, span(b)],
                own_row[:, span(b)].unsqueeze(1).to_broadcast([P, CHUNKS, P]),
                y_ps[b][:].rearrange("p (c t) -> p c t", c=CHUNKS),
                ALU.subtract,
            )

        law = tile("law", [P, 3, CHUNKS], F32, tag="h_raw1")
        for c in range(CHUNKS):
            nc.tensor.transpose(turn_ps[1][:, span(c)], picked[:, span(c)], ident[:])
        nc.scalar.copy(law[:], turn_ps[1][:].rearrange("p (c r) -> p r c", c=CHUNKS)[:, TABLE_ROWS, :])
        nn_col = [law[:, 0, c:c + 1] for c in range(CHUNKS)]
        isc_col = [law[:, 1, c:c + 1] for c in range(CHUNKS)]
        shp_col = [law[:, 2, c:c + 1] for c in range(CHUNKS)]

        exp_a = tiles("exp_a", CHUNKS, [P, V], F32)
        for b in range(BLOCKS):
            for c in range(CHUNKS):
                nc.scalar.activation(exp_a[c][:, span(b)], gap[:, c, span(b)], ACT.Exp, bias=nn_col[c])

        capped = tiles("capped", CHUNKS, [P, V], F32)
        soft = tiles("soft", CHUNKS, [P, V], F32)
        dis = tiles("dis", CHUNKS, [P, V], F32)
        log_dis = tiles("log_dis", CHUNKS, [P, V], F32)
        for c in range(CHUNKS):
            nc.vector.tensor_scalar(capped[c][:], exp_a[c][:], LN_CAP, None, ALU.min)
        for c in range(CHUNKS):
            nc.scalar.activation(soft[c][:], capped[c][:], ACT.Ln, bias=math.exp(SHIFT))
            nc.vector.scalar_tensor_tensor(dis[c][:], gap[:, c, :], nn_col[c], soft[c][:], ALU.add, ALU.max)
        for c in range(CHUNKS):
            nc.scalar.activation(log_dis[c][:], dis[c][:], ACT.Ln, scale=isc_col[c])

        twice_pos = tile("twice_pos", [P, BLOCKS, S], F32, tag="own_row")
        abs_y_sum = tile("abs_y_sum", [P, BLOCKS], F32)
        base = tile("base", [P, BLOCKS], F32)
        sum_ps = turn_ps[BLOCKS - 1]
        for b in range(BLOCKS):
            abs_y = tile("abs_y%d" % b, [P, S], F32, tag="capped%d" % b)
            nc.vector.tensor_scalar(twice_pos[:, b, :], y_ps[b][:], 0.0, 2.0, ALU.max, ALU.mult)
            nc.vector.tensor_tensor(abs_y[:], twice_pos[:, b, :], y_ps[b][:], ALU.subtract)
            for c in range(CHUNKS):
                nc.tensor.matmul(
                    sum_ps[:, span(b)], abs_y[:, span(c)], ident[:],
                    start=(c == 0), stop=(c == CHUNKS - 1), is_transpose=True,
                )
        nc.vector.tensor_reduce(
            abs_y_sum[:], sum_ps[:].rearrange("p (b j) -> p b j", b=BLOCKS), AXIS.X, ALU.add
        )
        nc.vector.tensor_scalar(base[:], abs_y_sum[:], 1.0 / UNK, None, ALU.add)

        power = tile("power", [P, CHUNKS, V], F32, tag="dis%d" % (CHUNKS - 1))
        keep = tiles("keep", BLOCKS, [P, S], F32)
        for group in LAW_GROUPS:
            samples = slice(group[0] * P, (group[-1] + 1) * P)
            for c in range(CHUNKS):
                nc.scalar.activation(power[:, c, samples], log_dis[c][:, samples], ACT.Exp, scale=shp_col[c])
            for b in group:
                nc.scalar.activation(
                    keep[b][:].rearrange("p (c t) -> p c t", c=CHUNKS), power[:, :, span(b)], ACT.Exp, scale=-1.0
                )

        kept = tiles("kept", BLOCKS, [P, S], F32)
        neg_yr = tiles("neg_yr", BLOCKS, [P, S + PAD], F32)
        neg_max = tiles("neg_max", BLOCKS, [P, 1], F32)
        minus_one = tile("minus_one", [P, 1], F32)
        nc.gpsimd.memset(minus_one[:], -1.0)
        for b in range(BLOCKS):
            nc.gpsimd.memset(neg_yr[b][:, S:S + 1], 0.0)
        for b in range(BLOCKS):
            nc.vector.tensor_tensor(kept[b][:], y_ps[b][:], keep[b][:], ALU.mult)
            for c in range(CHUNKS):
                nc.tensor.transpose(turn_ps[b][:, span(c)], kept[b][:, span(c)], ident[:])
            nc.vector.tensor_scalar(
                neg_yr[b][:, 0:S], turn_ps[b][:], -1.0, 0.0, ALU.mult, ALU.min, accum_out=neg_max[b][:]
            )

        er = tiles("er", BLOCKS, [P, S + PAD], F32)
        res = tiles("res", BLOCKS, [P, S], F32)
        total = tiles("total", BLOCKS, [P, 1], F32)
        abs_yr_sum = tiles("abs_yr_sum", BLOCKS, [P, 1], F32)
        denom = tiles("denom", BLOCKS, [P, 1], F32)
        inv_denom = tiles("inv_denom", BLOCKS, [P, 1], F32)
        for b in range(BLOCKS):
            early = b < EARLY_BLOCKS
            finisher = nc.gpsimd if early else nc.vector
            nc.scalar.activation(
                er[b][:, 0:S + 1], neg_yr[b][:, 0:S + 1], ACT.Exp,
                scale=-1.0, bias=neg_max[b][:], accum_out=total[b][:],
            )
            if early:
                abs_yr = tile("abs_yr%d" % b, [P, S], F32, tag="keep%d" % b)
                nc.scalar.activation(abs_yr[:], neg_yr[b][:, 0:S], ACT.Abs, accum_out=abs_yr_sum[b][:])
            else:
                nc.vector.tensor_reduce(
                    abs_yr_sum[b][:], neg_yr[b][:, 0:S], AXIS.X, ALU.add, apply_absolute_value=True
                )
            finisher.tensor_scalar(
                denom[b][:], base[:, b:b + 1], abs_yr_sum[b][:], total[b][:], ALU.subtract, ALU.mult
            )
            if early:
                nc.gpsimd.tensor_tensor(inv_denom[b][:], denom[b][:], minus_one[:], ALU.pow)
            else:
                nc.vector.reciprocal(inv_denom[b][:], denom[b][:])
            queues = (nc.sync, nc.scalar) if b == BLOCKS - 1 else (nc.sync,)
            for i, queue in enumerate(queues):
                classes = slice(i * S // len(queues), (i + 1) * S // len(queues))
                finisher.tensor_scalar(
                    res[b][:, classes], er[b][:, classes], inv_denom[b][:], 100.0 / UNK, ALU.mult, ALU.mult
                )
                queue.dma_start(out[span(b), classes], res[b][:, classes])
